import numpy as np
import ml_dtypes


def mxq(x, axis, fmt="e4m3"):
    dtype, down = {"e4m3": (ml_dtypes.float8_e4m3fn, 7), "e5m2": (ml_dtypes.float8_e5m2, 14)}[fmt]
    v = np.moveaxis(np.asarray(x, np.float32).astype(ml_dtypes.bfloat16).astype(np.float64), axis, -1)
    blocks = v.reshape(v.shape[:-1] + (-1, 32))
    amax = np.abs(blocks).max(-1, keepdims=True)
    byte = np.maximum(np.where(amax > 0, np.frexp(amax)[1] - 1 + 127, 0) - down, 1)
    scale = np.exp2(byte - 127.0)
    codes = (blocks / scale).astype(np.float32).astype(dtype).astype(np.float64)
    return np.moveaxis((codes * scale).reshape(v.shape), -1, axis)


WIDE = False


def mx_kscale(k):
    if not WIDE:
        return np.ones(k)
    levels = np.array([30, -30])
    if k % 512:
        return np.exp2(np.random.permutation(np.resize(levels, k // 32))).repeat(32)
    a = np.empty((k // 512, 16))
    for p in range(k // 512):
        a[p, :8] = np.random.permutation(np.resize(levels, 8))
        for g in range(8):
            far = levels[np.abs(levels - a[p, g]) >= 10]
            a[p, g + 8] = far[np.random.randint(len(far))]
    return np.exp2(a.ravel()).repeat(32)


def f64(x):
    return np.asarray(x).astype(np.float64)


def striped(idx):
    return np.tile(np.asarray(idx).reshape(-1, 16).T, (8, 1)).astype(np.uint16)


def unstriped(offs):
    return offs[:16].T.reshape(-1).astype(np.int64)


E2M1 = np.array([0.0, 0.5, 1.0, 1.5, 2.0, 3.0, 4.0, 6.0, -0.0, -0.5, -1.0, -1.5, -2.0, -3.0, -4.0, -6.0])


def pack_weight(w, fmt):
    k, n = w.shape
    w = f64(np.asarray(w, np.float32).astype(ml_dtypes.bfloat16)).reshape(k // 32, 32, n)
    amax = np.abs(w).max(1)
    if fmt in ("e4m3", "e5m2"):
        byte = np.frexp(amax)[1] - 1 + 127 - (7 if fmt == "e4m3" else 14)
    else:
        mant, ex = np.frexp(amax / 6.0)
        byte = np.where(mant > 0.5, ex, ex - 1) + 127
    byte = np.clip(np.where(amax > 0, byte, 1), 1, 254)
    scaled = (w * np.exp2(127.0 - byte)[:, None, :]).reshape(k, n).astype(np.float32)
    by_word = np.ascontiguousarray(scaled.reshape(k // 512, 128, 4, n).transpose(0, 1, 3, 2))
    if fmt in ("e4m3", "e5m2"):
        words = by_word.astype(ml_dtypes.float8_e4m3fn if fmt == "e4m3" else ml_dtypes.float8_e5m2).view(np.uint8)
    else:
        c = by_word.astype(ml_dtypes.float4_e2m1fn).view(np.uint8) & 0xF
        words = (c[..., 0::2] | (c[..., 1::2] << 4)).reshape(k // 512, 128, 2 * n)
    return np.ascontiguousarray(words), np.ascontiguousarray(byte.astype(np.uint8).reshape(k // 512, 16, n))


def unpack_weight(words, scales, fmt):
    g, _, n = scales.shape
    words = np.ascontiguousarray(words).reshape(g, 128, n, -1)
    if fmt in ("e4m3", "e5m2"):
        vals = words.view(ml_dtypes.float8_e4m3fn if fmt == "e4m3" else ml_dtypes.float8_e5m2).astype(np.float64)
    else:
        nib = np.empty((g, 128, n, 4), np.uint8)
        nib[..., 0::2] = words & 0xF
        nib[..., 1::2] = words >> 4
        vals = E2M1[nib]
    vals = vals * np.repeat(np.exp2(scales.astype(np.float64) - 127.0), 8, axis=1)[..., None]
    return vals.transpose(0, 1, 3, 2).reshape(g * 512, n)


def sigmoid(v):
    return 1.0 / (1.0 + np.exp(-v))


K, T, J, R, O, N, E = 512, 1024, 256, 512, 128, 256, 512


def setup_inputs():
    n = np.random.standard_normal
    idx = np.random.permutation(T)[:J]
    idx2 = np.random.permutation(J)[:O]
    idx3 = np.random.permutation(J)[:O]
    idx4 = np.random.permutation(J)[:O]
    idx5 = np.random.permutation(J)[:O]
    idx6 = np.random.permutation(E)[:O]
    idx7 = np.random.permutation(E)[:O]
    fk = mx_kscale(K)
    fr = mx_kscale(R)
    xtp = pack_weight(n((K, T)) / fk[:, None], "e4m3")
    wp = pack_weight(n((K, R)) * 1 / np.sqrt(K) * fk[:, None], "e2m1")
    w2p = pack_weight(n((K, R)) * 1 / np.sqrt(K) * fk[:, None], "e5m2")
    wbp = pack_weight(n((R, N)) * 1 / np.sqrt(R) / fr[:, None], "e5m2")
    return {
        "xt_words": xtp[0],
        "xt_scales": xtp[1],
        "w_words": wp[0],
        "w_scales": wp[1],
        "w2_words": w2p[0],
        "w2_scales": w2p[1],
        "sa": (np.random.uniform(0.5, 1.6, (R, 1)) * fr[:, None]).astype(np.float32),
        "sb": (np.random.uniform(0.5, 1.6, (R, 1)) * fr[:, None]).astype(np.float32),
        "bg": (np.random.uniform(-2.0, 2.0, (R, 1))).astype(np.float32),
        "bh": (np.random.uniform(-2.0, 2.0, (R, 1))).astype(np.float32),
        "wb_words": wbp[0],
        "wb_scales": wbp[1],
        "offs": striped(idx),
        "offs2": striped(idx2),
        "offs3": striped(idx3),
        "offs4": striped(idx4),
        "offs5": striped(idx5),
        "offs6": striped(idx6),
        "offs7": striped(idx7),
    }


def reference(xt_words, xt_scales, w_words, w_scales, w2_words, w2_scales, sa, sb, bg, bh, wb_words, wb_scales, offs, offs2, offs3, offs4, offs5, offs6, offs7):
    idx = unstriped(offs)
    idx2 = unstriped(offs2)
    idx3 = unstriped(offs3)
    idx4 = unstriped(offs4)
    idx5 = unstriped(offs5)
    idx6 = unstriped(offs6)
    idx7 = unstriped(offs7)
    xtu = unpack_weight(xt_words, xt_scales, "e4m3")
    wu = unpack_weight(w_words, w_scales, "e2m1")
    w2u = unpack_weight(w2_words, w2_scales, "e5m2")
    wbu = unpack_weight(wb_words, wb_scales, "e5m2")
    xtidxg = xtu[:, idx]
    a = wu.T @ xtidxg
    b = w2u.T @ xtidxg
    lb = b[:, 0:1]
    la = a[:, 0:1]
    u1 = a[:, idx2] * f64(sa) * sigmoid(a[:, idx3] * lb + f64(bg))
    u2 = b[:, idx4] * f64(sb) * sigmoid(b[:, idx5] * la + f64(bh))
    hid = np.maximum(u1, u2)
    hidq = mxq(hid, 0, "e4m3")
    p = wbu.T @ hidq
    pa = np.zeros((N, E))
    pa[:, idx6] = p
    pb = np.zeros((N, E))
    pb[:, idx7] = p
    y = pa + pb
    return y

@@ -1,0 +1,175 @@
+from contextlib import ExitStack
+
+import concourse.mybir as mybir
+
+K, T, J, R, O, N, E = 512, 1024, 256, 512, 128, 256, 512
+FLOPS = 2 * (2 * K * R * J) + 2 * R * N * O
+
+F32 = mybir.dt.float32
+BF16 = mybir.dt.bfloat16
+I32 = mybir.dt.int32
+U32 = mybir.dt.uint32
+U16 = mybir.dt.uint16
+U8 = mybir.dt.uint8
+E4M3 = mybir.dt.float8_e4m3fn_x4
+E5M2 = mybir.dt.float8_e5m2_x4
+E2M1 = mybir.dt.float4_e2m1fn_x4
+ACT = mybir.ActivationFunctionType
+ALU = mybir.AluOpType
+
+P = 128
+PACK = 4
+QUADS = 4
+
+
+def tile_list_slopeboth_twow_one_pagetwice_kernel(
+    tc, xt_words, xt_scales, w_words, w_scales, w2_words, w2_scales, sa, sb, bg, bh, wb_words, wb_scales,
+    offs, offs2, offs3, offs4, offs5, offs6, offs7, out,
+):
+    nc = tc.nc
+    with ExitStack() as ctx:
+        keep = ctx.enter_context(tc.tile_pool(name="keep", bufs=1))
+        psum = ctx.enter_context(tc.psum_pool(name="psum", bufs=8))
+
+        def sbuf(name, shape, dtype):
+            return keep.tile(shape, dtype, name=name, align_bytes=64)
+
+        def load_list(name, src):
+            tile = sbuf(name, list(src.shape), U16)
+            nc.sync.dma_start(tile[:], src)
+            return tile
+
+        def load_words(name, src, queue):
+            flat = src[0] if src.ndim == 3 else src[0].rearrange("p c t -> p (c t)")
+            tile = sbuf(name, [P, flat.shape[1]], U8)
+            queue.dma_start(tile[:].bitcast(I32), flat.bitcast(I32))
+            return tile
+
+        def zero_plane(name, cols):
+            plane = sbuf(name, [P, cols], U8)
+            nc.vector.memset(plane[:].bitcast(I32), 0)
+            return plane
+
+        def load_plane(plane, src):
+            for q in range(QUADS):
+                nc.sync.dma_start(plane[32 * q : 32 * q + 4, :].bitcast(I32), src[0, 4 * q : 4 * q + 4, :].bitcast(I32))
+
+        def load_rows(name, src):
+            cols = src.shape[2]
+            stage = sbuf(name, [4, QUADS, cols // 4], I32)
+            nc.sync.dma_start(stage[:], src[0].bitcast(I32).rearrange("(q r) c -> r q c", r=4))
+            return stage
+
+        def spread_rows(plane, stage):
+            for q in range(QUADS):
+                nc.vector.tensor_copy(plane[32 * q : 32 * q + 4, :].bitcast(I32), stage[:, q, :])
+
+        def load_features(name, src):
+            tile = sbuf(name, [P, PACK], F32)
+            nc.sync.dma_start(tile[:], src.rearrange("(p t) o -> p (t o)", t=PACK))
+            return tile
+
+        def deal(engine_copy, dst, src):
+            engine_copy(dst.rearrange("p (t m) -> p m t", t=PACK), src.rearrange("p (m t) -> p m t", t=PACK))
+
+        xs = zero_plane("xs", T)
+        o1 = load_list("o1", offs)
+        ws_rows = load_rows("ws_rows", w_scales)
+        xw = load_words("xw", xt_words, nc.sync)
+        load_plane(xs, xt_scales)
+        ww = load_words("ww", w_words, nc.sync)
+        w2w = load_words("w2w", w2_words, nc.sync)
+        w2s_rows = load_rows("w2s_rows", w2_scales)
+        o2 = load_list("o2", offs2)
+        sa_t = load_features("sa_t", sa)
+        o4 = load_list("o4", offs4)
+        sb_t = load_features("sb_t", sb)
+        o3 = load_list("o3", offs3)
+        bg_t = load_features("bg_t", bg)
+        o5 = load_list("o5", offs5)
+        bh_t = load_features("bh_t", bh)
+        ws = zero_plane("ws", R)
+        w2s = zero_plane("w2s", R)
+        wbs = zero_plane("wbs", N)
+        wbw = load_words("wbw", wb_words, nc.sync)
+        load_plane(wbs, wb_scales)
+        o6 = load_list("o6", offs6)
+        o7 = load_list("o7", offs7)
+
+        pages = []
+        for h in range(N // P):
+            pa = sbuf("pa%d" % h, [P, E], F32)
+            pb = sbuf("pb%d" % h, [P, E], F32)
+            nc.vector.memset(pa[:], 0.0)
+            nc.vector.memset(pb[:], 0.0)
+            pages.append((pa, pb))
+
+        spread_rows(ws, ws_rows)
+        gs = sbuf("gs", [P, J], U8)
+        nc.vector.tensor_copy(gs[:], xs[:].indirect(o1[:]))
+        ws_d = sbuf("ws_d", [P, R], U8)
+        deal(nc.vector.tensor_copy, ws_d[:], ws[:])
+        ww_d = sbuf("ww_d", [P, 2 * R], U8)
+        deal(nc.scalar.copy, ww_d[:].bitcast(U16), ww[:].bitcast(U16))
+        gw = sbuf("gw", [P, J], U32)
+        nc.vector.tensor_copy(gw[:], xw[:].bitcast(U32).indirect(o1[:]))
+
+        spread_rows(w2s, w2s_rows)
+        w2s_d = sbuf("w2s_d", [P, R], U8)
+        deal(nc.vector.tensor_copy, w2s_d[:], w2s[:])
+        w2w_d = sbuf("w2w_d", [P, R], U32)
+        deal(nc.scalar.copy, w2w_d[:], w2w[:].bitcast(U32))
+
+        def first_stage(name, lhs, lhs_scale):
+            bank = psum.tile([P, J], F32, name="bank")
+            nc.tensor.matmul_mx(out=bank[:], lhsT=lhs, lhsT_scale=lhs_scale, rhs=gw[:].bitcast(E4M3), rhs_scale=gs[:],
+                                start=True, stop=True)
+            rows = sbuf(name, [P, J], F32)
+            nc.vector.tensor_copy(rows[:], bank[:])
+            return rows
+
+        a = [first_stage("a%d" % t, ww_d[:, 2 * P * t : 2 * P * (t + 1)].bitcast(E2M1), ws_d[:, P * t : P * (t + 1)])
+             for t in range(PACK)]
+        b = [first_stage("b%d" % t, w2w_d[:, P * t : P * (t + 1)].bitcast(E5M2), w2s_d[:, P * t : P * (t + 1)])
+             for t in range(PACK)]
+
+        vals = [sbuf("val%d" % t, [P, 2, O], F32) for t in range(PACK)]
+        gates = [sbuf("gate%d" % t, [P, 2, O], F32) for t in range(PACK)]
+        for t in range(PACK):
+            nc.scalar.activation(out=vals[t][:, 0, :], in_=a[t][:].indirect(o2[:]), func=ACT.Copy, scale=sa_t[:, t : t + 1])
+        for t in range(PACK):
+            nc.scalar.activation(out=vals[t][:, 1, :], in_=b[t][:].indirect(o4[:]), func=ACT.Copy, scale=sb_t[:, t : t + 1])
+        hid16 = sbuf("hid16", [P, O, PACK], BF16)
+        for t in range(PACK):
+            nc.scalar.activation(out=gates[t][:, 0, :], in_=a[t][:].indirect(o3[:]), func=ACT.Sigmoid,
+                                 scale=b[t][:, 0:1], bias=bg_t[:, t : t + 1])
+            nc.scalar.activation(out=gates[t][:, 1, :], in_=b[t][:].indirect(o5[:]), func=ACT.Sigmoid,
+                                 scale=a[t][:, 0:1], bias=bh_t[:, t : t + 1])
+            u = sbuf("u%d" % t, [P, 2, O], F32)
+            for s in range(2):
+                nc.vector.tensor_tensor(u[:, s, :], vals[t][:, s, :], gates[t][:, s, :], ALU.mult)
+            nc.vector.tensor_tensor(hid16[:, :, t], u[:, 0, :], u[:, 1, :], ALU.max)
+
+        hw = sbuf("hw", [P, O], U32)
+        hs = sbuf("hs", [P, O], U8)
+        nc.vector.quantize_mx(out=hw[:].bitcast(E4M3), scales=hs[:], in_=hid16[:].rearrange("p o t -> p (o t)"))
+
+        ps = []
+        for h in range(N // P):
+            bank = psum.tile([P, O], F32, name="bank")
+            nc.tensor.matmul_mx(out=bank[:], lhsT=wbw[:, 4 * P * h : 4 * P * (h + 1)].bitcast(E5M2),
+                                lhsT_scale=wbs[:, P * h : P * (h + 1)], rhs=hw[:].bitcast(E4M3), rhs_scale=hs[:],
+                                start=True, stop=True)
+            p = sbuf("p%d" % h, [P, O], F32)
+            copy = nc.vector.tensor_copy if h == 0 else nc.scalar.copy
+            copy(p[:], bank[:])
+            ps.append(p)
+        for h in range(N // P):
+            pa, pb = pages[h]
+            nc.vector.tensor_copy(pa[:].indirect(o6[:]), ps[h][:])
+            nc.scalar.activation(out=pb[:].indirect(o7[:]), in_=ps[h][:], func=ACT.Copy)
+        for h in range(N // P):
+            pa, pb = pages[h]
+            y = sbuf("y%d" % h, [P, E], F32)
+            nc.vector.tensor_tensor(y[:], pa[:], pb[:], ALU.add)
+            nc.sync.dma_start(out[P * h : P * (h + 1), :], y[:])

@@ -96,6 +96,11 @@ def tile_list_slopeboth_twow_one_pagetwice_kernel(
         o6 = load_list("o6", offs6)
         o7 = load_list("o7", offs7)
 
+        warm_in = sbuf("warm_in", [P, 1], F32)
+        warm_out = sbuf("warm_out", [P, 1], F32)
+        nc.gpsimd.memset(warm_in[:], 0.0)
+        nc.scalar.activation(out=warm_out[:], in_=warm_in[:], func=ACT.Sigmoid)
+
         pages = []
         for h in range(N // P):
             pa = sbuf("pa%d" % h, [P, E], F32)

@@ -50,9 +50,9 @@ def tile_list_slopeboth_twow_one_pagetwice_kernel(
             nc.vector.memset(plane[:].bitcast(I32), 0)
             return plane
 
-        def load_plane(plane, src):
+        def load_plane(plane, src, queue):
             for q in range(QUADS):
-                nc.sync.dma_start(plane[32 * q : 32 * q + 4, :].bitcast(I32), src[0, 4 * q : 4 * q + 4, :].bitcast(I32))
+                queue.dma_start(plane[32 * q : 32 * q + 4, :].bitcast(I32), src[0, 4 * q : 4 * q + 4, :].bitcast(I32))
 
         def load_rows(name, src):
             cols = src.shape[2]
@@ -76,7 +76,7 @@ def tile_list_slopeboth_twow_one_pagetwice_kernel(
         o1 = load_list("o1", offs)
         ws_rows = load_rows("ws_rows", w_scales)
         xw = load_words("xw", xt_words, nc.sync)
-        load_plane(xs, xt_scales)
+        load_plane(xs, xt_scales, nc.sync)
         ww = load_words("ww", w_words, nc.sync)
         w2w = load_words("w2w", w2_words, nc.sync)
         w2s_rows = load_rows("w2s_rows", w2_scales)
@@ -92,7 +92,7 @@ def tile_list_slopeboth_twow_one_pagetwice_kernel(
         w2s = zero_plane("w2s", R)
         wbs = zero_plane("wbs", N)
         wbw = load_words("wbw", wb_words, nc.sync)
-        load_plane(wbs, wb_scales)
+        load_plane(wbs, wb_scales, nc.sync)
         o6 = load_list("o6", offs6)
         o7 = load_list("o7", offs7)
 
@@ -109,51 +109,78 @@ def tile_list_slopeboth_twow_one_pagetwice_kernel(
             nc.vector.memset(pb[:], 0.0)
             pages.append((pa, pb))
 
+        def deal_scales(dst, src, t0, t1):
+            nc.vector.tensor_copy(dst[:].rearrange("p (t m) -> p t m", t=PACK)[:, t0:t1, :],
+                                  src[:].rearrange("p (m t) -> p t m", t=PACK)[:, t0:t1, :])
+
+        def first_stage(name, lhs, lhs_scale, copy, width=J):
+            rows = sbuf(name, [P, J], F32)
+            for c0 in range(0, J, width):
+                cols = slice(c0, c0 + width)
+                bank = psum.tile([P, width], F32, name="bank")
+                nc.tensor.matmul_mx(out=bank[:], lhsT=lhs, lhsT_scale=lhs_scale, rhs=gw[:, cols].bitcast(E4M3),
+                                    rhs_scale=gs[:, cols], start=True, stop=True)
+                copy(rows[:, cols], bank[:])
+            return rows
+
+        def rows_a(t, copy, width=J):
+            return first_stage("a%d" % t, ww_d[:, 2 * P * t : 2 * P * (t + 1)].bitcast(E2M1), ws_d[:, P * t : P * (t + 1)],
+                               copy, width)
+
+        def rows_b(t):
+            return first_stage("b%d" % t, w2w_d[:, P * t : P * (t + 1)].bitcast(E5M2), w2s_d[:, P * t : P * (t + 1)],
+                               nc.vector.tensor_copy)
+
         spread_rows(ws, ws_rows)
-        gs = sbuf("gs", [P, J], U8)
-        nc.vector.tensor_copy(gs[:], xs[:].indirect(o1[:]))
         ws_d = sbuf("ws_d", [P, R], U8)
-        deal(nc.vector.tensor_copy, ws_d[:], ws[:])
+        deal_scales(ws_d, ws, 0, 1)
         ww_d = sbuf("ww_d", [P, 2 * R], U8)
         deal(nc.scalar.copy, ww_d[:].bitcast(U16), ww[:].bitcast(U16))
         gw = sbuf("gw", [P, J], U32)
         nc.vector.tensor_copy(gw[:], xw[:].bitcast(U32).indirect(o1[:]))
+        gs = sbuf("gs", [P, J], U8)
+        for c in range(2):
+            nc.vector.tensor_copy(gs[:, P * c : P * (c + 1)], xs[:].indirect(o1[:, 8 * c : 8 * (c + 1)]))
+        deal_scales(ws_d, ws, 1, PACK)
+        w2w_d = sbuf("w2w_d", [P, R], U32)
+        deal(nc.scalar.copy, w2w_d[:], w2w[:].bitcast(U32))
+        a = [rows_a(0, nc.scalar.copy, P)]
 
         spread_rows(w2s, w2s_rows)
         w2s_d = sbuf("w2s_d", [P, R], U8)
-        deal(nc.vector.tensor_copy, w2s_d[:], w2s[:])
-        w2w_d = sbuf("w2w_d", [P, R], U32)
-        deal(nc.scalar.copy, w2w_d[:], w2w[:].bitcast(U32))
-
-        def first_stage(name, lhs, lhs_scale):
-            bank = psum.tile([P, J], F32, name="bank")
-            nc.tensor.matmul_mx(out=bank[:], lhsT=lhs, lhsT_scale=lhs_scale, rhs=gw[:].bitcast(E4M3), rhs_scale=gs[:],
-                                start=True, stop=True)
-            rows = sbuf(name, [P, J], F32)
-            nc.vector.tensor_copy(rows[:], bank[:])
-            return rows
-
-        a = [first_stage("a%d" % t, ww_d[:, 2 * P * t : 2 * P * (t + 1)].bitcast(E2M1), ws_d[:, P * t : P * (t + 1)])
-             for t in range(PACK)]
-        b = [first_stage("b%d" % t, w2w_d[:, P * t : P * (t + 1)].bitcast(E5M2), w2s_d[:, P * t : P * (t + 1)])
-             for t in range(PACK)]
+        deal_scales(w2s_d, w2s, 0, 1)
+        a.extend(rows_a(t, nc.vector.tensor_copy) for t in range(1, PACK))
+        b = [rows_b(0)]
+        deal_scales(w2s_d, w2s, 1, PACK)
+        b.extend(rows_b(t) for t in range(1, PACK))
 
         vals = [sbuf("val%d" % t, [P, 2, O], F32) for t in range(PACK)]
         gates = [sbuf("gate%d" % t, [P, 2, O], F32) for t in range(PACK)]
         for t in range(PACK):
             nc.scalar.activation(out=vals[t][:, 0, :], in_=a[t][:].indirect(o2[:]), func=ACT.Copy, scale=sa_t[:, t : t + 1])
+        hid16 = sbuf("hid16", [P, O, PACK], BF16)
+        hid = sbuf("hid", [P, 2, O], F32)
         for t in range(PACK):
             nc.scalar.activation(out=vals[t][:, 1, :], in_=b[t][:].indirect(o4[:]), func=ACT.Copy, scale=sb_t[:, t : t + 1])
-        hid16 = sbuf("hid16", [P, O, PACK], BF16)
-        for t in range(PACK):
             nc.scalar.activation(out=gates[t][:, 0, :], in_=a[t][:].indirect(o3[:]), func=ACT.Sigmoid,
                                  scale=b[t][:, 0:1], bias=bg_t[:, t : t + 1])
-            nc.scalar.activation(out=gates[t][:, 1, :], in_=b[t][:].indirect(o5[:]), func=ACT.Sigmoid,
-                                 scale=a[t][:, 0:1], bias=bh_t[:, t : t + 1])
+            width = O if t < PACK - 1 else O // 2
+            pieces = [slice(c0, c0 + width) for c0 in range(0, O, width)]
+            for c in pieces:
+                nc.scalar.activation(out=gates[t][:, 1, c], in_=b[t][:].indirect(o5[:, c.start // 16 : c.stop // 16]),
+                                     func=ACT.Sigmoid, scale=a[t][:, 0:1], bias=bh_t[:, t : t + 1])
             u = sbuf("u%d" % t, [P, 2, O], F32)
-            for s in range(2):
-                nc.vector.tensor_tensor(u[:, s, :], vals[t][:, s, :], gates[t][:, s, :], ALU.mult)
-            nc.vector.tensor_tensor(hid16[:, :, t], u[:, 0, :], u[:, 1, :], ALU.max)
+            if t < 2:
+                nc.vector.tensor_tensor(u[:], vals[t][:], gates[t][:], ALU.mult)
+                nc.vector.tensor_tensor(hid[:, t, :], u[:, 0, :], u[:, 1, :], ALU.max)
+            else:
+                nc.vector.tensor_tensor(u[:, 0, :], vals[t][:, 0, :], gates[t][:, 0, :], ALU.mult)
+                for c in pieces:
+                    nc.vector.tensor_tensor(u[:, 1, c], vals[t][:, 1, c], gates[t][:, 1, c], ALU.mult)
+                for c in pieces:
+                    nc.vector.tensor_tensor(hid16[:, c, t], u[:, 0, c], u[:, 1, c], ALU.max)
+            if t == 1:
+                nc.vector.tensor_copy(hid16[:, :, 0:2], hid[:].rearrange("p t o -> p o t"))
 
         hw = sbuf("hw", [P, O], U32)
         hs = sbuf("hs", [P, O], U8)
@@ -169,12 +196,22 @@ def tile_list_slopeboth_twow_one_pagetwice_kernel(
             copy = nc.vector.tensor_copy if h == 0 else nc.scalar.copy
             copy(p[:], bank[:])
             ps.append(p)
-        for h in range(N // P):
-            pa, pb = pages[h]
-            nc.vector.tensor_copy(pa[:].indirect(o6[:]), ps[h][:])
-            nc.scalar.activation(out=pb[:].indirect(o7[:]), in_=ps[h][:], func=ACT.Copy)
-        for h in range(N // P):
+
+        def put_scalar(page, offsets, values):
+            nc.scalar.activation(out=page[:].indirect(offsets), in_=values, func=ACT.Copy)
+
+        def put_vector(page, offsets, values):
+            nc.vector.tensor_copy(page[:].indirect(offsets), values)
+
+        def add_and_store(h):
             pa, pb = pages[h]
             y = sbuf("y%d" % h, [P, E], F32)
-            nc.vector.tensor_tensor(y[:], pa[:], pb[:], ALU.add)
-            nc.sync.dma_start(out[P * h : P * (h + 1), :], y[:])
+            for cols, queue in ((slice(0, E // 2), nc.sync), (slice(E // 2, E), nc.scalar)):
+                nc.vector.tensor_tensor(y[:, cols], pa[:, cols], pb[:, cols], ALU.add)
+                queue.dma_start(out[P * h : P * (h + 1), cols], y[:, cols])
+
+        for h in range(N // P):
+            put_vector(pages[h][0], o6[:], ps[h][:])
+            put_scalar(pages[h][1], o7[:], ps[h][:])
+        for h in range(N // P):
+            add_and_store(h)

@@ -20,6 +20,17 @@ ALU = mybir.AluOpType
 P = 128
 PACK = 4
 QUADS = 4
+ROWS = 4
+PER_COL = 16
+EARLY = 2
+
+
+def halves(n):
+    return [slice(0, n // 2), slice(n // 2, n)]
+
+
+def entries(offsets, part):
+    return offsets[:, part.start // PER_COL : part.stop // PER_COL]
 
 
 def tile_list_slopeboth_twow_one_pagetwice_kernel(
@@ -31,18 +42,18 @@ def tile_list_slopeboth_twow_one_pagetwice_kernel(
         keep = ctx.enter_context(tc.tile_pool(name="keep", bufs=1))
         psum = ctx.enter_context(tc.psum_pool(name="psum", bufs=8))
 
-        def sbuf(name, shape, dtype):
-            return keep.tile(shape, dtype, name=name, align_bytes=64)
+        def sbuf(name, shape, dtype, buffer_of=""):
+            return keep.tile(shape, dtype, name=name, tag=buffer_of or name, align_bytes=64)
 
         def load_list(name, src):
             tile = sbuf(name, list(src.shape), U16)
             nc.sync.dma_start(tile[:], src)
             return tile
 
-        def load_words(name, src, queue):
+        def load_words(name, src):
             flat = src[0] if src.ndim == 3 else src[0].rearrange("p c t -> p (c t)")
             tile = sbuf(name, [P, flat.shape[1]], U8)
-            queue.dma_start(tile[:].bitcast(I32), flat.bitcast(I32))
+            nc.sync.dma_start(tile[:].bitcast(I32), flat.bitcast(I32))
             return tile
 
         def zero_plane(name, cols):
@@ -50,49 +61,53 @@ def tile_list_slopeboth_twow_one_pagetwice_kernel(
             nc.vector.memset(plane[:].bitcast(I32), 0)
             return plane
 
-        def load_plane(plane, src, queue):
+        def load_plane(plane, src):
             for q in range(QUADS):
-                queue.dma_start(plane[32 * q : 32 * q + 4, :].bitcast(I32), src[0, 4 * q : 4 * q + 4, :].bitcast(I32))
+                rows = src[0, ROWS * q : ROWS * (q + 1), :]
+                nc.sync.dma_start(plane[32 * q : 32 * q + ROWS, :].bitcast(I32), rows.bitcast(I32))
 
         def load_rows(name, src):
-            cols = src.shape[2]
-            stage = sbuf(name, [4, QUADS, cols // 4], I32)
-            nc.sync.dma_start(stage[:], src[0].bitcast(I32).rearrange("(q r) c -> r q c", r=4))
+            stage = sbuf(name, [ROWS, QUADS, src.shape[2] // 4], I32)
+            nc.sync.dma_start(stage[:], src[0].bitcast(I32).rearrange("(q i) c -> i q c", i=ROWS))
             return stage
 
         def spread_rows(plane, stage):
             for q in range(QUADS):
-                nc.vector.tensor_copy(plane[32 * q : 32 * q + 4, :].bitcast(I32), stage[:, q, :])
+                nc.vector.tensor_copy(plane[32 * q : 32 * q + ROWS, :].bitcast(I32), stage[:, q, :])
 
         def load_features(name, src):
             tile = sbuf(name, [P, PACK], F32)
             nc.sync.dma_start(tile[:], src.rearrange("(p t) o -> p (t o)", t=PACK))
             return tile
 
-        def deal(engine_copy, dst, src):
-            engine_copy(dst.rearrange("p (t m) -> p m t", t=PACK), src.rearrange("p (m t) -> p m t", t=PACK))
+        def deal_words(dst, src):
+            nc.scalar.copy(dst.rearrange("p (t m) -> p m t", t=PACK), src.rearrange("p (m t) -> p m t", t=PACK))
+
+        def deal_scales(dst, src, t0, t1):
+            nc.vector.tensor_copy(dst[:].rearrange("p (t m) -> p t m", t=PACK)[:, t0:t1, :],
+                                  src[:].rearrange("p (m t) -> p t m", t=PACK)[:, t0:t1, :])
 
         xs = zero_plane("xs", T)
         o1 = load_list("o1", offs)
         ws_rows = load_rows("ws_rows", w_scales)
-        xw = load_words("xw", xt_words, nc.sync)
-        load_plane(xs, xt_scales, nc.sync)
-        ww = load_words("ww", w_words, nc.sync)
-        w2w = load_words("w2w", w2_words, nc.sync)
+        xw = load_words("xw", xt_words)
+        load_plane(xs, xt_scales)
+        ww = load_words("ww", w_words)
+        w2w = load_words("w2w", w2_words)
         w2s_rows = load_rows("w2s_rows", w2_scales)
         o2 = load_list("o2", offs2)
         sa_t = load_features("sa_t", sa)
-        o4 = load_list("o4", offs4)
-        sb_t = load_features("sb_t", sb)
         o3 = load_list("o3", offs3)
         bg_t = load_features("bg_t", bg)
+        o4 = load_list("o4", offs4)
+        sb_t = load_features("sb_t", sb)
         o5 = load_list("o5", offs5)
         bh_t = load_features("bh_t", bh)
         ws = zero_plane("ws", R)
         w2s = zero_plane("w2s", R)
         wbs = zero_plane("wbs", N)
-        wbw = load_words("wbw", wb_words, nc.sync)
-        load_plane(wbs, wb_scales, nc.sync)
+        wbw = load_words("wbw", wb_words)
+        load_plane(wbs, wb_scales)
         o6 = load_list("o6", offs6)
         o7 = load_list("o7", offs7)
 
@@ -109,109 +124,96 @@ def tile_list_slopeboth_twow_one_pagetwice_kernel(
             nc.vector.memset(pb[:], 0.0)
             pages.append((pa, pb))
 
-        def deal_scales(dst, src, t0, t1):
-            nc.vector.tensor_copy(dst[:].rearrange("p (t m) -> p t m", t=PACK)[:, t0:t1, :],
-                                  src[:].rearrange("p (m t) -> p t m", t=PACK)[:, t0:t1, :])
-
-        def first_stage(name, lhs, lhs_scale, copy, width=J):
+        def first_stage(name, lhs, lhs_scale, copy, parts):
             rows = sbuf(name, [P, J], F32)
-            for c0 in range(0, J, width):
-                cols = slice(c0, c0 + width)
-                bank = psum.tile([P, width], F32, name="bank")
+            for cols in parts:
+                bank = psum.tile([P, cols.stop - cols.start], F32, name="bank")
                 nc.tensor.matmul_mx(out=bank[:], lhsT=lhs, lhsT_scale=lhs_scale, rhs=gw[:, cols].bitcast(E4M3),
                                     rhs_scale=gs[:, cols], start=True, stop=True)
                 copy(rows[:, cols], bank[:])
             return rows
 
-        def rows_a(t, copy, width=J):
-            return first_stage("a%d" % t, ww_d[:, 2 * P * t : 2 * P * (t + 1)].bitcast(E2M1), ws_d[:, P * t : P * (t + 1)],
-                               copy, width)
+        def rows_a(t, copy, parts):
+            lhs = ww_d[:, 2 * P * t : 2 * P * (t + 1)].bitcast(E2M1)
+            return first_stage("a%d" % t, lhs, ws_d[:, P * t : P * (t + 1)], copy, parts)
 
         def rows_b(t):
-            return first_stage("b%d" % t, w2w_d[:, P * t : P * (t + 1)].bitcast(E5M2), w2s_d[:, P * t : P * (t + 1)],
-                               nc.vector.tensor_copy)
+            lhs = w2w_d[:, P * t : P * (t + 1)].bitcast(E5M2)
+            return first_stage("b%d" % t, lhs, w2s_d[:, P * t : P * (t + 1)], nc.vector.tensor_copy, [slice(0, J)])
 
         spread_rows(ws, ws_rows)
         ws_d = sbuf("ws_d", [P, R], U8)
         deal_scales(ws_d, ws, 0, 1)
         ww_d = sbuf("ww_d", [P, 2 * R], U8)
-        deal(nc.scalar.copy, ww_d[:].bitcast(U16), ww[:].bitcast(U16))
+        deal_words(ww_d[:].bitcast(U16), ww[:].bitcast(U16))
         gw = sbuf("gw", [P, J], U32)
         nc.vector.tensor_copy(gw[:], xw[:].bitcast(U32).indirect(o1[:]))
         gs = sbuf("gs", [P, J], U8)
-        for c in range(2):
-            nc.vector.tensor_copy(gs[:, P * c : P * (c + 1)], xs[:].indirect(o1[:, 8 * c : 8 * (c + 1)]))
+        for part in halves(J):
+            nc.vector.tensor_copy(gs[:, part], xs[:].indirect(entries(o1, part)))
         deal_scales(ws_d, ws, 1, PACK)
         w2w_d = sbuf("w2w_d", [P, R], U32)
-        deal(nc.scalar.copy, w2w_d[:], w2w[:].bitcast(U32))
-        a = [rows_a(0, nc.scalar.copy, P)]
+        deal_words(w2w_d[:], w2w[:].bitcast(U32))
+        a = [rows_a(0, nc.scalar.copy, halves(J))]
 
         spread_rows(w2s, w2s_rows)
         w2s_d = sbuf("w2s_d", [P, R], U8)
         deal_scales(w2s_d, w2s, 0, 1)
-        a.extend(rows_a(t, nc.vector.tensor_copy) for t in range(1, PACK))
+        a.extend(rows_a(t, nc.vector.tensor_copy, [slice(0, J)]) for t in range(1, PACK))
         b = [rows_b(0)]
         deal_scales(w2s_d, w2s, 1, PACK)
         b.extend(rows_b(t) for t in range(1, PACK))
 
-        vals = [sbuf("val%d" % t, [P, 2, O], F32) for t in range(PACK)]
-        gates = [sbuf("gate%d" % t, [P, 2, O], F32) for t in range(PACK)]
+        val_a = sbuf("val_a", [P, PACK, O], F32)
         for t in range(PACK):
-            nc.scalar.activation(out=vals[t][:, 0, :], in_=a[t][:].indirect(o2[:]), func=ACT.Copy, scale=sa_t[:, t : t + 1])
+            nc.scalar.activation(out=val_a[:, t, :], in_=a[t][:].indirect(o2[:]), func=ACT.Copy, scale=sa_t[:, t : t + 1])
+
         hid16 = sbuf("hid16", [P, O, PACK], BF16)
-        hid = sbuf("hid", [P, 2, O], F32)
+        hid_early = sbuf("hid_early", [P, EARLY, O], F32)
         for t in range(PACK):
-            nc.scalar.activation(out=vals[t][:, 1, :], in_=b[t][:].indirect(o4[:]), func=ACT.Copy, scale=sb_t[:, t : t + 1])
-            nc.scalar.activation(out=gates[t][:, 0, :], in_=a[t][:].indirect(o3[:]), func=ACT.Sigmoid,
+            val_b = sbuf("val_b%d" % t, [P, O], F32, "a%d" % (t - 2) if t >= 2 else "")
+            gates = sbuf("gates%d" % t, [P, 2, O], F32, "b%d" % (t - 2) if t >= 2 else "")
+            gate_a, gate_b = gates[:, 0, :], gates[:, 1, :]
+            nc.scalar.activation(out=gate_a, in_=a[t][:].indirect(o3[:]), func=ACT.Sigmoid,
                                  scale=b[t][:, 0:1], bias=bg_t[:, t : t + 1])
-            width = O if t < PACK - 1 else O // 2
-            pieces = [slice(c0, c0 + width) for c0 in range(0, O, width)]
-            for c in pieces:
-                nc.scalar.activation(out=gates[t][:, 1, c], in_=b[t][:].indirect(o5[:, c.start // 16 : c.stop // 16]),
-                                     func=ACT.Sigmoid, scale=a[t][:, 0:1], bias=bh_t[:, t : t + 1])
+            nc.scalar.activation(out=val_b[:], in_=b[t][:].indirect(o4[:]), func=ACT.Copy, scale=sb_t[:, t : t + 1])
+            parts = halves(O) if t == PACK - 1 else [slice(0, O)]
+            for part in parts:
+                nc.scalar.activation(out=gate_b[:, part], in_=b[t][:].indirect(entries(o5, part)), func=ACT.Sigmoid,
+                                     scale=a[t][:, 0:1], bias=bh_t[:, t : t + 1])
             u = sbuf("u%d" % t, [P, 2, O], F32)
-            if t < 2:
-                nc.vector.tensor_tensor(u[:], vals[t][:], gates[t][:], ALU.mult)
-                nc.vector.tensor_tensor(hid[:, t, :], u[:, 0, :], u[:, 1, :], ALU.max)
-            else:
-                nc.vector.tensor_tensor(u[:, 0, :], vals[t][:, 0, :], gates[t][:, 0, :], ALU.mult)
-                for c in pieces:
-                    nc.vector.tensor_tensor(u[:, 1, c], vals[t][:, 1, c], gates[t][:, 1, c], ALU.mult)
-                for c in pieces:
-                    nc.vector.tensor_tensor(hid16[:, c, t], u[:, 0, c], u[:, 1, c], ALU.max)
-            if t == 1:
-                nc.vector.tensor_copy(hid16[:, :, 0:2], hid[:].rearrange("p t o -> p o t"))
+            nc.vector.tensor_tensor(u[:, 0, :], val_a[:, t, :], gate_a, ALU.mult)
+            for part in parts:
+                nc.vector.tensor_tensor(u[:, 1, part], val_b[:, part], gate_b[:, part], ALU.mult)
+            for part in parts:
+                dst = hid_early[:, t, part] if t < EARLY else hid16[:, part, t]
+                nc.vector.tensor_tensor(dst, u[:, 0, part], u[:, 1, part], ALU.max)
+            if t == EARLY - 1:
+                nc.vector.tensor_copy(hid16[:, :, 0:EARLY], hid_early[:].rearrange("p t o -> p o t"))
 
         hw = sbuf("hw", [P, O], U32)
         hs = sbuf("hs", [P, O], U8)
-        nc.vector.quantize_mx(out=hw[:].bitcast(E4M3), scales=hs[:], in_=hid16[:].rearrange("p o t -> p (o t)"))
+        for part in halves(O):
+            nc.vector.quantize_mx(out=hw[:, part].bitcast(E4M3), scales=hs[:, part],
+                                  in_=hid16[:, part, :].rearrange("p o t -> p (o t)"))
 
-        ps = []
-        for h in range(N // P):
+        p_rows = []
+        for h, copy in enumerate((nc.vector.tensor_copy, nc.scalar.copy)):
             bank = psum.tile([P, O], F32, name="bank")
-            nc.tensor.matmul_mx(out=bank[:], lhsT=wbw[:, 4 * P * h : 4 * P * (h + 1)].bitcast(E5M2),
+            nc.tensor.matmul_mx(out=bank[:], lhsT=wbw[:, PACK * P * h : PACK * P * (h + 1)].bitcast(E5M2),
                                 lhsT_scale=wbs[:, P * h : P * (h + 1)], rhs=hw[:].bitcast(E4M3), rhs_scale=hs[:],
                                 start=True, stop=True)
-            p = sbuf("p%d" % h, [P, O], F32)
-            copy = nc.vector.tensor_copy if h == 0 else nc.scalar.copy
-            copy(p[:], bank[:])
-            ps.append(p)
+            rows = sbuf("p%d" % h, [P, O], F32)
+            copy(rows[:], bank[:])
+            p_rows.append(rows)
 
-        def put_scalar(page, offsets, values):
-            nc.scalar.activation(out=page[:].indirect(offsets), in_=values, func=ACT.Copy)
+        for (pa, pb), rows in zip(pages, p_rows):
+            nc.vector.tensor_copy(pa[:].indirect(o6[:]), rows[:])
+            nc.scalar.activation(out=pb[:].indirect(o7[:]), in_=rows[:], func=ACT.Copy)
 
-        def put_vector(page, offsets, values):
-            nc.vector.tensor_copy(page[:].indirect(offsets), values)
-
-        def add_and_store(h):
-            pa, pb = pages[h]
+        for h, (pa, pb) in enumerate(pages):
             y = sbuf("y%d" % h, [P, E], F32)
-            for cols, queue in ((slice(0, E // 2), nc.sync), (slice(E // 2, E), nc.scalar)):
-                nc.vector.tensor_tensor(y[:, cols], pa[:, cols], pb[:, cols], ALU.add)
+            for cols, queue in zip(halves(E), (nc.sync, nc.scalar)):
+                adder = nc.gpsimd if h == 0 and cols.start == 0 else nc.vector
+                adder.tensor_tensor(y[:, cols], pa[:, cols], pb[:, cols], ALU.add)
                 queue.dma_start(out[P * h : P * (h + 1), cols], y[:, cols])
-
-        for h in range(N // P):
-            put_vector(pages[h][0], o6[:], ps[h][:])
-            put_scalar(pages[h][1], o7[:], ps[h][:])
-        for h in range(N // P):
-            add_and_store(h)

@@ -214,6 +214,5 @@ def tile_list_slopeboth_twow_one_pagetwice_kernel(
         for h, (pa, pb) in enumerate(pages):
             y = sbuf("y%d" % h, [P, E], F32)
             for cols, queue in zip(halves(E), (nc.sync, nc.scalar)):
-                adder = nc.gpsimd if h == 0 and cols.start == 0 else nc.vector
-                adder.tensor_tensor(y[:, cols], pa[:, cols], pb[:, cols], ALU.add)
+                nc.vector.tensor_tensor(y[:, cols], pa[:, cols], pb[:, cols], ALU.add)
                 queue.dma_start(out[P * h : P * (h + 1), cols], y[:, cols])

from contextlib import ExitStack

import concourse.mybir as mybir

K, T, J, R, O, N, E = 512, 1024, 256, 512, 128, 256, 512
FLOPS = 2 * (2 * K * R * J) + 2 * R * N * O

F32 = mybir.dt.float32
BF16 = mybir.dt.bfloat16
I32 = mybir.dt.int32
U32 = mybir.dt.uint32
U16 = mybir.dt.uint16
U8 = mybir.dt.uint8
E4M3 = mybir.dt.float8_e4m3fn_x4
E5M2 = mybir.dt.float8_e5m2_x4
E2M1 = mybir.dt.float4_e2m1fn_x4
ACT = mybir.ActivationFunctionType
ALU = mybir.AluOpType

P = 128
PACK = 4
QUADS = 4
ROWS = 4
PER_COL = 16
EARLY = 2


def halves(n):
    return [slice(0, n // 2), slice(n // 2, n)]


def entries(offsets, part):
    return offsets[:, part.start // PER_COL : part.stop // PER_COL]


def tile_list_slopeboth_twow_one_pagetwice_kernel(
    tc, xt_words, xt_scales, w_words, w_scales, w2_words, w2_scales, sa, sb, bg, bh, wb_words, wb_scales,
    offs, offs2, offs3, offs4, offs5, offs6, offs7, out,
):
    nc = tc.nc
    with ExitStack() as ctx:
        keep = ctx.enter_context(tc.tile_pool(name="keep", bufs=1))
        psum = ctx.enter_context(tc.psum_pool(name="psum", bufs=8))

        def sbuf(name, shape, dtype, buffer_of=""):
            return keep.tile(shape, dtype, name=name, tag=buffer_of or name, align_bytes=64)

        def load_list(name, src):
            tile = sbuf(name, list(src.shape), U16)
            nc.sync.dma_start(tile[:], src)
            return tile

        def load_words(name, src):
            flat = src[0] if src.ndim == 3 else src[0].rearrange("p c t -> p (c t)")
            tile = sbuf(name, [P, flat.shape[1]], U8)
            nc.sync.dma_start(tile[:].bitcast(I32), flat.bitcast(I32))
            return tile

        def zero_plane(name, cols):
            plane = sbuf(name, [P, cols], U8)
            nc.vector.memset(plane[:].bitcast(I32), 0)
            return plane

        def load_plane(plane, src):
            for q in range(QUADS):
                rows = src[0, ROWS * q : ROWS * (q + 1), :]
                nc.sync.dma_start(plane[32 * q : 32 * q + ROWS, :].bitcast(I32), rows.bitcast(I32))

        def load_rows(name, src):
            stage = sbuf(name, [ROWS, QUADS, src.shape[2] // 4], I32)
            nc.sync.dma_start(stage[:], src[0].bitcast(I32).rearrange("(q i) c -> i q c", i=ROWS))
            return stage

        def spread_rows(plane, stage):
            for q in range(QUADS):
                nc.vector.tensor_copy(plane[32 * q : 32 * q + ROWS, :].bitcast(I32), stage[:, q, :])

        def load_features(name, src):
            tile = sbuf(name, [P, PACK], F32)
            nc.sync.dma_start(tile[:], src.rearrange("(p t) o -> p (t o)", t=PACK))
            return tile

        def deal_words(dst, src):
            nc.scalar.copy(dst.rearrange("p (t m) -> p m t", t=PACK), src.rearrange("p (m t) -> p m t", t=PACK))

        def deal_scales(dst, src, t0, t1):
            nc.vector.tensor_copy(dst[:].rearrange("p (t m) -> p t m", t=PACK)[:, t0:t1, :],
                                  src[:].rearrange("p (m t) -> p t m", t=PACK)[:, t0:t1, :])

        xs = zero_plane("xs", T)
        o1 = load_list("o1", offs)
        ws_rows = load_rows("ws_rows", w_scales)
        xw = load_words("xw", xt_words)
        load_plane(xs, xt_scales)
        ww = load_words("ww", w_words)
        w2w = load_words("w2w", w2_words)
        w2s_rows = load_rows("w2s_rows", w2_scales)
        o2 = load_list("o2", offs2)
        sa_t = load_features("sa_t", sa)
        o3 = load_list("o3", offs3)
        bg_t = load_features("bg_t", bg)
        o4 = load_list("o4", offs4)
        sb_t = load_features("sb_t", sb)
        o5 = load_list("o5", offs5)
        bh_t = load_features("bh_t", bh)
        ws = zero_plane("ws", R)
        w2s = zero_plane("w2s", R)
        wbs = zero_plane("wbs", N)
        wbw = load_words("wbw", wb_words)
        load_plane(wbs, wb_scales)
        o6 = load_list("o6", offs6)
        o7 = load_list("o7", offs7)

        warm_in = sbuf("warm_in", [P, 1], F32)
        warm_out = sbuf("warm_out", [P, 1], F32)
        nc.gpsimd.memset(warm_in[:], 0.0)
        nc.scalar.activation(out=warm_out[:], in_=warm_in[:], func=ACT.Sigmoid)

        pages = []
        for h in range(N // P):
            pa = sbuf("pa%d" % h, [P, E], F32)
            pb = sbuf("pb%d" % h, [P, E], F32)
            nc.vector.memset(pa[:], 0.0)
            nc.vector.memset(pb[:], 0.0)
            pages.append((pa, pb))

        def first_stage(name, lhs, lhs_scale, copy, parts):
            rows = sbuf(name, [P, J], F32)
            for cols in parts:
                bank = psum.tile([P, cols.stop - cols.start], F32, name="bank")
                nc.tensor.matmul_mx(out=bank[:], lhsT=lhs, lhsT_scale=lhs_scale, rhs=gw[:, cols].bitcast(E4M3),
                                    rhs_scale=gs[:, cols], start=True, stop=True)
                copy(rows[:, cols], bank[:])
            return rows

        def rows_a(t, copy, parts):
            lhs = ww_d[:, 2 * P * t : 2 * P * (t + 1)].bitcast(E2M1)
            return first_stage("a%d" % t, lhs, ws_d[:, P * t : P * (t + 1)], copy, parts)

        def rows_b(t):
            lhs = w2w_d[:, P * t : P * (t + 1)].bitcast(E5M2)
            return first_stage("b%d" % t, lhs, w2s_d[:, P * t : P * (t + 1)], nc.vector.tensor_copy, [slice(0, J)])

        spread_rows(ws, ws_rows)
        ws_d = sbuf("ws_d", [P, R], U8)
        deal_scales(ws_d, ws, 0, 1)
        ww_d = sbuf("ww_d", [P, 2 * R], U8)
        deal_words(ww_d[:].bitcast(U16), ww[:].bitcast(U16))
        gw = sbuf("gw", [P, J], U32)
        nc.vector.tensor_copy(gw[:], xw[:].bitcast(U32).indirect(o1[:]))
        gs = sbuf("gs", [P, J], U8)
        for part in halves(J):
            nc.vector.tensor_copy(gs[:, part], xs[:].indirect(entries(o1, part)))
        deal_scales(ws_d, ws, 1, PACK)
        w2w_d = sbuf("w2w_d", [P, R], U32)
        deal_words(w2w_d[:], w2w[:].bitcast(U32))
        a = [rows_a(0, nc.scalar.copy, halves(J))]

        spread_rows(w2s, w2s_rows)
        w2s_d = sbuf("w2s_d", [P, R], U8)
        deal_scales(w2s_d, w2s, 0, 1)
        a.extend(rows_a(t, nc.vector.tensor_copy, [slice(0, J)]) for t in range(1, PACK))
        b = [rows_b(0)]
        deal_scales(w2s_d, w2s, 1, PACK)
        b.extend(rows_b(t) for t in range(1, PACK))

        val_a = sbuf("val_a", [P, PACK, O], F32)
        for t in range(PACK):
            nc.scalar.activation(out=val_a[:, t, :], in_=a[t][:].indirect(o2[:]), func=ACT.Copy, scale=sa_t[:, t : t + 1])

        hid16 = sbuf("hid16", [P, O, PACK], BF16)
        hid_early = sbuf("hid_early", [P, EARLY, O], F32)
        for t in range(PACK):
            val_b = sbuf("val_b%d" % t, [P, O], F32, "a%d" % (t - 2) if t >= 2 else "")
            gates = sbuf("gates%d" % t, [P, 2, O], F32, "b%d" % (t - 2) if t >= 2 else "")
            gate_a, gate_b = gates[:, 0, :], gates[:, 1, :]
            nc.scalar.activation(out=gate_a, in_=a[t][:].indirect(o3[:]), func=ACT.Sigmoid,
                                 scale=b[t][:, 0:1], bias=bg_t[:, t : t + 1])
            nc.scalar.activation(out=val_b[:], in_=b[t][:].indirect(o4[:]), func=ACT.Copy, scale=sb_t[:, t : t + 1])
            parts = halves(O) if t == PACK - 1 else [slice(0, O)]
            for part in parts:
                nc.scalar.activation(out=gate_b[:, part], in_=b[t][:].indirect(entries(o5, part)), func=ACT.Sigmoid,
                                     scale=a[t][:, 0:1], bias=bh_t[:, t : t + 1])
            u = sbuf("u%d" % t, [P, 2, O], F32)
            nc.vector.tensor_tensor(u[:, 0, :], val_a[:, t, :], gate_a, ALU.mult)
            for part in parts:
                nc.vector.tensor_tensor(u[:, 1, part], val_b[:, part], gate_b[:, part], ALU.mult)
            for part in parts:
                dst = hid_early[:, t, part] if t < EARLY else hid16[:, part, t]
                nc.vector.tensor_tensor(dst, u[:, 0, part], u[:, 1, part], ALU.max)
            if t == EARLY - 1:
                nc.vector.tensor_copy(hid16[:, :, 0:EARLY], hid_early[:].rearrange("p t o -> p o t"))

        hw = sbuf("hw", [P, O], U32)
        hs = sbuf("hs", [P, O], U8)
        for part in halves(O):
            nc.vector.quantize_mx(out=hw[:, part].bitcast(E4M3), scales=hs[:, part],
                                  in_=hid16[:, part, :].rearrange("p o t -> p (o t)"))

        p_rows = []
        for h, copy in enumerate((nc.vector.tensor_copy, nc.scalar.copy)):
            bank = psum.tile([P, O], F32, name="bank")
            nc.tensor.matmul_mx(out=bank[:], lhsT=wbw[:, PACK * P * h : PACK * P * (h + 1)].bitcast(E5M2),
                                lhsT_scale=wbs[:, P * h : P * (h + 1)], rhs=hw[:].bitcast(E4M3), rhs_scale=hs[:],
                                start=True, stop=True)
            rows = sbuf("p%d" % h, [P, O], F32)
            copy(rows[:], bank[:])
            p_rows.append(rows)

        for (pa, pb), rows in zip(pages, p_rows):
            nc.vector.tensor_copy(pa[:].indirect(o6[:]), rows[:])
            nc.scalar.activation(out=pb[:].indirect(o7[:]), in_=rows[:], func=ACT.Copy)

        for h, (pa, pb) in enumerate(pages):
            y = sbuf("y%d" % h, [P, E], F32)
            for cols, queue in zip(halves(E), (nc.sync, nc.scalar)):
                nc.vector.tensor_tensor(y[:, cols], pa[:, cols], pb[:, cols], ALU.add)
                queue.dma_start(out[P * h : P * (h + 1), cols], y[:, cols])
